import numpy as np
import ml_dtypes


def mxq(x, axis, fmt="e4m3"):
    dtype, down = {"e4m3": (ml_dtypes.float8_e4m3fn, 7), "e5m2": (ml_dtypes.float8_e5m2, 14)}[fmt]
    v = np.moveaxis(np.asarray(x, np.float32).astype(ml_dtypes.bfloat16).astype(np.float64), axis, -1)
    blocks = v.reshape(v.shape[:-1] + (-1, 32))
    amax = np.abs(blocks).max(-1, keepdims=True)
    byte = np.maximum(np.where(amax > 0, np.frexp(amax)[1] - 1 + 127, 0) - down, 1)
    scale = np.exp2(byte - 127.0)
    codes = (blocks / scale).astype(np.float32).astype(dtype).astype(np.float64)
    return np.moveaxis((codes * scale).reshape(v.shape), -1, axis)


WIDE = False


def mx_kscale(k):
    if not WIDE:
        return np.ones(k)
    levels = np.array([10, -10, 5, -5, 0])
    if k % 512:
        return np.exp2(np.random.permutation(np.resize(levels, k // 32))).repeat(32)
    a = np.empty((k // 512, 16))
    for p in range(k // 512):
        a[p, :8] = np.random.permutation(np.resize(levels, 8))
        for g in range(8):
            far = levels[np.abs(levels - a[p, g]) >= 10]
            a[p, g + 8] = far[np.random.randint(len(far))]
    return np.exp2(a.ravel()).repeat(32)


def f64(x):
    return np.asarray(x).astype(np.float64)


def striped(idx):
    return np.tile(idx.reshape(-1, 16).T, (8, 1)).astype(np.uint16)


def unstriped(offs):
    return offs[:16].T.reshape(-1).astype(np.int64)


E2M1 = np.array([0.0, 0.5, 1.0, 1.5, 2.0, 3.0, 4.0, 6.0, -0.0, -0.5, -1.0, -1.5, -2.0, -3.0, -4.0, -6.0])


def pack_weight(w, fmt):
    k, n = w.shape
    w = f64(np.asarray(w, np.float32).astype(ml_dtypes.bfloat16)).reshape(k // 32, 32, n)
    amax = np.abs(w).max(1)
    if fmt == "e4m3":
        byte = np.frexp(amax)[1] - 1 + 127 - 7
    else:
        mant, ex = np.frexp(amax / 6.0)
        byte = np.where(mant > 0.5, ex, ex - 1) + 127
    byte = np.clip(np.where(amax > 0, byte, 1), 1, 254)
    scaled = (w * np.exp2(127.0 - byte)[:, None, :]).reshape(k, n).astype(np.float32)
    by_word = np.ascontiguousarray(scaled.reshape(k // 512, 128, 4, n).transpose(0, 1, 3, 2))
    if fmt == "e4m3":
        words = by_word.astype(ml_dtypes.float8_e4m3fn).view(np.uint8)
    else:
        c = by_word.astype(ml_dtypes.float4_e2m1fn).view(np.uint8) & 0xF
        words = (c[..., 0::2] | (c[..., 1::2] << 4)).reshape(k // 512, 128, 2 * n)
    return np.ascontiguousarray(words), np.ascontiguousarray(byte.astype(np.uint8).reshape(k // 512, 16, n))


def unpack_weight(words, scales, fmt):
    g, _, n = scales.shape
    words = np.ascontiguousarray(words).reshape(g, 128, n, -1)
    if fmt == "e4m3":
        vals = words.view(ml_dtypes.float8_e4m3fn).astype(np.float64)
    else:
        nib = np.empty((g, 128, n, 4), np.uint8)
        nib[..., 0::2] = words & 0xF
        nib[..., 1::2] = words >> 4
        vals = E2M1[nib]
    vals = vals * np.repeat(np.exp2(scales.astype(np.float64) - 127.0), 8, axis=1)[..., None]
    return vals.transpose(0, 1, 3, 2).reshape(g * 512, n)


def relu(v):
    return np.maximum(v, 0.0)


K, T, S, H, N = 1024, 1024, 512, 512, 256


def setup_inputs():
    n = np.random.standard_normal
    s = mx_kscale(K)
    u = mx_kscale(H)
    hard = np.random.permutation(T)[:S]
    x = pack_weight(n((K, T)) * s[:, None], "e4m3")
    w = pack_weight(n((K, N)) / np.sqrt(K) / s[:, None], "e4m3")
    return {
        "x_words": x[0],
        "x_scales": x[1],
        "w_words": w[0],
        "w_scales": w[1],
        "w1": (n((K, H)) / np.sqrt(K) / s[:, None] * u).astype(np.float32),
        "w2": (n((H, N)) / np.sqrt(H) / u[:, None]).astype(np.float32),
        "offs": striped(hard),
    }


def reference(x_words, x_scales, w_words, w_scales, w1, w2, offs):
    w = unpack_weight(w_words, w_scales, "e4m3")
    w1q = mxq(f64(w1), 0, "e4m3")
    w2q = mxq(f64(w2), 0, "e4m3")
    idx = unstriped(offs)
    x = unpack_weight(x_words, x_scales, "e4m3")
    out = w.T @ x
    h = relu(w1q.T @ x[:, idx])
    out[:, idx] = w2q.T @ mxq(h, 0, "e4m3")
    return out

@@ -1,0 +1,186 @@
+from contextlib import ExitStack
+
+import concourse.mybir as mybir
+
+K, T, S, H, N = 1024, 1024, 512, 512, 256
+FLOPS = 2 * K * N * T + 2 * K * H * S + 2 * H * N * S
+
+F32 = mybir.dt.float32
+BF16 = mybir.dt.bfloat16
+I32 = mybir.dt.int32
+U32 = mybir.dt.uint32
+U16 = mybir.dt.uint16
+U8 = mybir.dt.uint8
+FP8X4 = mybir.dt.float8_e4m3fn_x4
+COPY = mybir.ActivationFunctionType.Copy
+RELU = mybir.ActivationFunctionType.Relu
+
+P = 128
+PACK = 4
+PASSES = 2
+CHUNK = 128
+HALF = 256
+
+
+def tile_moe_cas_mlp_relu_kernel(tc, x_words, x_scales, w_words, w_scales, w1, w2, offs, out):
+    nc = tc.nc
+    with ExitStack() as ctx:
+        keep = ctx.enter_context(tc.tile_pool(name="keep", bufs=1))
+        psum = ctx.enter_context(tc.psum_pool(name="psum", bufs=8))
+
+        offsets = keep.tile([P, S // 16], U16, name="offsets")
+        xw = [keep.tile([P, T], I32, name="xw%d" % s, align_bytes=64) for s in range(PASSES)]
+        xs = keep.tile([P, T], U8, name="xs", align_bytes=64)
+        ww = keep.tile([P, PASSES, N], I32, name="ww", align_bytes=64)
+        ws = keep.tile([P, N], U8, name="ws", align_bytes=64)
+        w1_raw0 = keep.tile([P, PACK, H], F32, name="w1_raw0", align_bytes=64)
+        w1_raw1 = [keep.tile([P, PACK, HALF], F32, name="w1_raw1%d" % h, align_bytes=64) for h in range(2)]
+        w2_raw = keep.tile([P, PACK, N], F32, name="w2_raw", align_bytes=64)
+        w1_bf = [keep.tile([P, PACK, P, PACK], BF16, name="w1_bf%d" % s, align_bytes=64) for s in range(PASSES)]
+        w1_codes = [keep.tile([P, H], U32, name="w1_codes%d" % s, align_bytes=64) for s in range(PASSES)]
+        w1_sc = [keep.tile([P, H], U8, name="w1_sc%d" % s, align_bytes=64) for s in range(PASSES)]
+        w2_bf = keep.tile([P, N, PACK], BF16, name="w2_bf", align_bytes=64)
+        w2_codes = keep.tile([P, N], U32, name="w2_codes", align_bytes=64)
+        w2_sc = keep.tile([P, N], U8, name="w2_sc", align_bytes=64)
+        gw = [keep.tile([P, S], U32, name="gw%d" % s, align_bytes=64) for s in range(PASSES)]
+        gs = keep.tile([P, S], U8, name="gs", align_bytes=64)
+        h_bf = [keep.tile([P, CHUNK, PACK], BF16, name="h_bf%d" % c, align_bytes=64) for c in range(S // CHUNK)]
+        h_codes = keep.tile([P, S], U32, name="h_codes", align_bytes=64)
+        h_sc = keep.tile([P, S], U8, name="h_sc", align_bytes=64)
+        z = [keep.tile([P, S], F32, name="z%d" % u, align_bytes=64) for u in range(2)]
+        res = [keep.tile([P, T], F32, name="res%d" % u, align_bytes=64) for u in range(2)]
+
+        nc.vector.memset(xs[:].bitcast(I32), 0)
+        nc.vector.memset(ws[:].bitcast(I32), 0)
+
+        def load_x(s):
+            nc.sync.dma_start(out=xw[s][:], in_=x_words[s].rearrange("p t d -> p (t d)").bitcast(I32))
+
+        def load_scales(tile, src):
+            for q in range(4):
+                nc.sync.dma_start(out=tile[32 * q : 32 * q + 8, :].bitcast(I32), in_=src[:, 4 * q : 4 * q + 4, :].bitcast(I32))
+
+        w1_rows = w1.rearrange("(s p j) c -> s p j c", s=PASSES, j=PACK)
+        load_x(0)
+        nc.sync.dma_start(out=offsets[:], in_=offs)
+        load_scales(xs, x_scales)
+        load_x(1)
+        nc.sync.dma_start(out=w1_raw0[:], in_=w1_rows[0])
+        load_scales(ws, w_scales)
+        nc.sync.dma_start(out=ww[:], in_=w_words.rearrange("s p n d -> p s (n d)").bitcast(I32))
+        for h in range(2):
+            nc.sync.dma_start(out=w1_raw1[h][:], in_=w1_rows[1][:, :, h * HALF : (h + 1) * HALF])
+        nc.sync.dma_start(out=w2_raw[:], in_=w2.rearrange("(p j) n -> p j n", j=PACK))
+
+        def cast_w1(engine, s, raw, c_raw, c0, c1):
+            dst = w1_bf[s][:, :, c0 // PACK : c1 // PACK, :].rearrange("p t m j -> p m j t")
+            src = raw[:, :, c0 - c_raw : c1 - c_raw].rearrange("p j (m t) -> p m j t", t=PACK)
+            if engine == "scalar":
+                nc.scalar.activation(out=dst, in_=src, func=COPY)
+            else:
+                nc.vector.tensor_copy(out=dst, in_=src)
+
+        def quantize_w1_half(s, h):
+            for t in range(PACK):
+                m0, m1 = h * 64, (h + 1) * 64
+                cols = slice(t * P + m0, t * P + m1)
+                nc.vector.quantize_mx(
+                    out=w1_codes[s][:, cols].bitcast(FP8X4),
+                    scales=w1_sc[s][:, cols],
+                    in_=w1_bf[s][:, t, m0:m1, :].rearrange("p m j -> p (m j)"),
+                )
+
+        nc.vector.tensor_copy(out=gw[0][:], in_=xw[0][:].bitcast(U32).indirect(offsets[:]))
+        nc.vector.tensor_copy(out=gs[:], in_=xs[:].indirect(offsets[:]))
+        nc.vector.tensor_copy(out=gw[1][:], in_=xw[1][:].bitcast(U32).indirect(offsets[:]))
+
+        cast_w1("scalar", 0, w1_raw0, 0, 0, 256)
+        cast_w1("vector", 0, w1_raw0, 0, 256, 512)
+
+        for u in range(2):
+            for g in range(2):
+                acc = psum.tile([P, 512], F32, name="acc")
+                cols = slice(g * 512, (g + 1) * 512)
+                for s in range(PASSES):
+                    nc.tensor.matmul_mx(
+                        out=acc[:],
+                        lhsT=ww[:, s, u * P : (u + 1) * P].bitcast(FP8X4),
+                        lhsT_scale=ws[4 * s : P, u * P : (u + 1) * P],
+                        rhs=xw[s][:, cols].bitcast(FP8X4),
+                        rhs_scale=xs[4 * s : P, cols],
+                        start=(s == 0),
+                        stop=(s == PASSES - 1),
+                    )
+                nc.scalar.activation(out=res[u][:, cols], in_=acc[:], func=COPY)
+
+        nc.vector.quantize_mx(
+            out=w1_codes[0][:].bitcast(FP8X4),
+            scales=w1_sc[0][:],
+            in_=w1_bf[0][:].rearrange("p t m j -> p (t m j)"),
+        )
+        cast_w1("vector", 1, w1_raw1[0], 0, 0, 256)
+        quantize_w1_half(1, 0)
+        cast_w1("vector", 1, w1_raw1[1], 256, 256, 432)
+        cast_w1("scalar", 1, w1_raw1[1], 256, 432, 512)
+        quantize_w1_half(1, 1)
+
+        nc.vector.tensor_copy(
+            out=w2_bf[:].rearrange("p (c i) j -> p c j i", i=PACK),
+            in_=w2_raw[:].rearrange("p j (c i) -> p c j i", i=PACK),
+        )
+        nc.vector.quantize_mx(out=w2_codes[:].bitcast(FP8X4), scales=w2_sc[:], in_=w2_bf[:].rearrange("p n j -> p (n j)"))
+
+        def first(c):
+            slots = slice(c * CHUNK, (c + 1) * CHUNK)
+            acc = psum.tile([P, PACK, CHUNK], F32, name="acc")
+            for t in range(PACK):
+                for s in range(PASSES):
+                    nc.tensor.matmul_mx(
+                        out=acc[:, t, :],
+                        lhsT=w1_codes[s][:, t * P : (t + 1) * P].bitcast(FP8X4),
+                        lhsT_scale=w1_sc[s][:, t * P : (t + 1) * P],
+                        rhs=gw[s][:, slots].bitcast(FP8X4),
+                        rhs_scale=gs[4 * s : P, slots],
+                        start=(s == 0),
+                        stop=(s == PASSES - 1),
+                    )
+            nc.scalar.activation(out=h_bf[c][:], in_=acc[:].rearrange("p t n -> p n t"), func=RELU)
+
+        def quantize_h(c):
+            slots = slice(c * CHUNK, (c + 1) * CHUNK)
+            nc.vector.quantize_mx(
+                out=h_codes[:, slots].bitcast(FP8X4), scales=h_sc[:, slots], in_=h_bf[c][:].rearrange("p n t -> p (n t)")
+            )
+
+        def second(u, a, b):
+            acc = psum.tile([P, b - a], F32, name="acc")
+            nc.tensor.matmul_mx(
+                out=acc[:],
+                lhsT=w2_codes[:, u * P : (u + 1) * P].bitcast(FP8X4),
+                lhsT_scale=w2_sc[:, u * P : (u + 1) * P],
+                rhs=h_codes[:, a:b].bitcast(FP8X4),
+                rhs_scale=h_sc[:, a:b],
+                start=True,
+                stop=True,
+            )
+            nc.scalar.activation(out=z[u][:, a:b], in_=acc[:], func=COPY)
+
+        def scatter(u, a, b):
+            nc.vector.tensor_copy(out=res[u][:].indirect(offsets[:, a // 16 : b // 16]), in_=z[u][:, a:b])
+
+        chunks = S // CHUNK
+        first(0)
+        for c in range(chunks):
+            if c + 1 < chunks:
+                first(c + 1)
+            quantize_h(c)
+            second(0, c * CHUNK, (c + 1) * CHUNK)
+            if c > 0:
+                scatter(0, (c - 1) * CHUNK, c * CHUNK)
+            if c % 2 == 1:
+                second(1, (c - 1) * CHUNK, (c + 1) * CHUNK)
+        scatter(0, S - CHUNK, S)
+        nc.sync.dma_start(out=out[0:P, :], in_=res[0][:])
+        for h in range(2):
+            scatter(1, h * HALF, (h + 1) * HALF)
+        nc.sync.dma_start(out=out[P : 2 * P, :], in_=res[1][:])

@@ -33,10 +33,10 @@ def tile_moe_cas_mlp_relu_kernel(tc, x_words, x_scales, w_words, w_scales, w1, w
         xs = keep.tile([P, T], U8, name="xs", align_bytes=64)
         ww = keep.tile([P, PASSES, N], I32, name="ww", align_bytes=64)
         ws = keep.tile([P, N], U8, name="ws", align_bytes=64)
-        w1_raw0 = keep.tile([P, PACK, H], F32, name="w1_raw0", align_bytes=64)
-        w1_raw1 = [keep.tile([P, PACK, HALF], F32, name="w1_raw1%d" % h, align_bytes=64) for h in range(2)]
+        w1_raw = [[keep.tile([P, PACK, HALF], F32, name="w1_raw%d%d" % (s, h), tag="slab%d%d" % (s, h), align_bytes=64) for h in range(2)] for s in range(PASSES)]
         w2_raw = keep.tile([P, PACK, N], F32, name="w2_raw", align_bytes=64)
-        w1_bf = [keep.tile([P, PACK, P, PACK], BF16, name="w1_bf%d" % s, align_bytes=64) for s in range(PASSES)]
+        w1_bf0 = keep.tile([P, PACK, P, PACK], BF16, name="w1_bf0", align_bytes=64)
+        w1_bf1 = [keep.tile([P, PACK, 64, PACK], BF16, name="w1_bf1%d" % h, align_bytes=64) for h in range(2)]
         w1_codes = [keep.tile([P, H], U32, name="w1_codes%d" % s, align_bytes=64) for s in range(PASSES)]
         w1_sc = [keep.tile([P, H], U8, name="w1_sc%d" % s, align_bytes=64) for s in range(PASSES)]
         w2_bf = keep.tile([P, N, PACK], BF16, name="w2_bf", align_bytes=64)
@@ -48,7 +48,6 @@ def tile_moe_cas_mlp_relu_kernel(tc, x_words, x_scales, w_words, w_scales, w1, w
         h_codes = keep.tile([P, S], U32, name="h_codes", align_bytes=64)
         h_sc = keep.tile([P, S], U8, name="h_sc", align_bytes=64)
         z = [keep.tile([P, S], F32, name="z%d" % u, align_bytes=64) for u in range(2)]
-        res = [keep.tile([P, T], F32, name="res%d" % u, align_bytes=64) for u in range(2)]
 
         nc.vector.memset(xs[:].bitcast(I32), 0)
         nc.vector.memset(ws[:].bitcast(I32), 0)
@@ -61,44 +60,40 @@ def tile_moe_cas_mlp_relu_kernel(tc, x_words, x_scales, w_words, w_scales, w1, w
                 nc.sync.dma_start(out=tile[32 * q : 32 * q + 8, :].bitcast(I32), in_=src[:, 4 * q : 4 * q + 4, :].bitcast(I32))
 
         w1_rows = w1.rearrange("(s p j) c -> s p j c", s=PASSES, j=PACK)
+        def load_w1(s, h):
+            nc.sync.dma_start(out=w1_raw[s][h][:], in_=w1_rows[s][:, :, h * HALF : (h + 1) * HALF])
+
         load_x(0)
         nc.sync.dma_start(out=offsets[:], in_=offs)
         load_scales(xs, x_scales)
+        load_w1(0, 0)
         load_x(1)
-        nc.sync.dma_start(out=w1_raw0[:], in_=w1_rows[0])
+        load_w1(0, 1)
         load_scales(ws, w_scales)
         nc.sync.dma_start(out=ww[:], in_=w_words.rearrange("s p n d -> p s (n d)").bitcast(I32))
-        for h in range(2):
-            nc.sync.dma_start(out=w1_raw1[h][:], in_=w1_rows[1][:, :, h * HALF : (h + 1) * HALF])
+        load_w1(1, 0)
+        load_w1(1, 1)
         nc.sync.dma_start(out=w2_raw[:], in_=w2.rearrange("(p j) n -> p j n", j=PACK))
 
-        def cast_w1(engine, s, raw, c_raw, c0, c1):
-            dst = w1_bf[s][:, :, c0 // PACK : c1 // PACK, :].rearrange("p t m j -> p m j t")
-            src = raw[:, :, c0 - c_raw : c1 - c_raw].rearrange("p j (m t) -> p m j t", t=PACK)
+        def cast_w1(engine, dst, raw, t0, t1):
+            dst = dst[:, t0:t1, :, :].rearrange("p t m j -> p m j t")
+            src = raw[:].rearrange("p j (m t) -> p m j t", t=PACK)[:, :, :, t0:t1]
             if engine == "scalar":
                 nc.scalar.activation(out=dst, in_=src, func=COPY)
             else:
                 nc.vector.tensor_copy(out=dst, in_=src)
 
-        def quantize_w1_half(s, h):
+        def quantize_w1_half(h):
             for t in range(PACK):
-                m0, m1 = h * 64, (h + 1) * 64
-                cols = slice(t * P + m0, t * P + m1)
+                cols = slice(t * P + h * 64, t * P + (h + 1) * 64)
                 nc.vector.quantize_mx(
-                    out=w1_codes[s][:, cols].bitcast(FP8X4),
-                    scales=w1_sc[s][:, cols],
-                    in_=w1_bf[s][:, t, m0:m1, :].rearrange("p m j -> p (m j)"),
+                    out=w1_codes[1][:, cols].bitcast(FP8X4),
+                    scales=w1_sc[1][:, cols],
+                    in_=w1_bf1[h][:, t, :, :].rearrange("p m j -> p (m j)"),
                 )
 
-        nc.vector.tensor_copy(out=gw[0][:], in_=xw[0][:].bitcast(U32).indirect(offsets[:]))
-        nc.vector.tensor_copy(out=gs[:], in_=xs[:].indirect(offsets[:]))
-        nc.vector.tensor_copy(out=gw[1][:], in_=xw[1][:].bitcast(U32).indirect(offsets[:]))
-
-        cast_w1("scalar", 0, w1_raw0, 0, 0, 256)
-        cast_w1("vector", 0, w1_raw0, 0, 256, 512)
-
-        for u in range(2):
-            for g in range(2):
+        def light(u, g):
+            if True:
                 acc = psum.tile([P, 512], F32, name="acc")
                 cols = slice(g * 512, (g + 1) * 512)
                 for s in range(PASSES):
@@ -113,16 +108,26 @@ def tile_moe_cas_mlp_relu_kernel(tc, x_words, x_scales, w_words, w_scales, w1, w
                     )
                 nc.scalar.activation(out=res[u][:, cols], in_=acc[:], func=COPY)
 
+        def cast_shared(dst, raw):
+            cast_w1("vector", dst, raw, 0, 2)
+            cast_w1("scalar", dst, raw, 2, 4)
+
+        nc.vector.tensor_copy(out=gw[0][:], in_=xw[0][:].bitcast(U32).indirect(offsets[:]))
+        nc.vector.tensor_copy(out=gs[:], in_=xs[:].indirect(offsets[:]))
+        cast_w1("scalar", w1_bf0[:, :, 0:64, :], w1_raw[0][0], 0, 4)
+        nc.vector.tensor_copy(out=gw[1][:], in_=xw[1][:].bitcast(U32).indirect(offsets[:]))
+        cast_shared(w1_bf0[:, :, 64:128, :], w1_raw[0][1])
         nc.vector.quantize_mx(
             out=w1_codes[0][:].bitcast(FP8X4),
             scales=w1_sc[0][:],
-            in_=w1_bf[0][:].rearrange("p t m j -> p (t m j)"),
+            in_=w1_bf0[:].rearrange("p t m j -> p (t m j)"),
         )
-        cast_w1("vector", 1, w1_raw1[0], 0, 0, 256)
-        quantize_w1_half(1, 0)
-        cast_w1("vector", 1, w1_raw1[1], 256, 256, 432)
-        cast_w1("scalar", 1, w1_raw1[1], 256, 432, 512)
-        quantize_w1_half(1, 1)
+        for h in range(2):
+            cast_shared(w1_bf1[h][:], w1_raw[1][h])
+            quantize_w1_half(h)
+        res = [keep.tile([P, T], F32, name="res%d" % u, tag=("slab11", "res1")[u], align_bytes=64) for u in range(2)]
+        light(0, 0)
+        light(0, 1)
 
         nc.vector.tensor_copy(
             out=w2_bf[:].rearrange("p (c i) j -> p c j i", i=PACK),
@@ -152,7 +157,7 @@ def tile_moe_cas_mlp_relu_kernel(tc, x_words, x_scales, w_words, w_scales, w1, w
                 out=h_codes[:, slots].bitcast(FP8X4), scales=h_sc[:, slots], in_=h_bf[c][:].rearrange("p n t -> p (n t)")
             )
 
-        def second(u, a, b):
+        def second(u, a, b, engine="scalar"):
             acc = psum.tile([P, b - a], F32, name="acc")
             nc.tensor.matmul_mx(
                 out=acc[:],
@@ -163,24 +168,29 @@ def tile_moe_cas_mlp_relu_kernel(tc, x_words, x_scales, w_words, w_scales, w1, w
                 start=True,
                 stop=True,
             )
-            nc.scalar.activation(out=z[u][:, a:b], in_=acc[:], func=COPY)
+            if engine == "scalar":
+                nc.scalar.activation(out=z[u][:, a:b], in_=acc[:], func=COPY)
+            else:
+                nc.vector.tensor_copy(out=z[u][:, a:b], in_=acc[:])
 
         def scatter(u, a, b):
             nc.vector.tensor_copy(out=res[u][:].indirect(offsets[:, a // 16 : b // 16]), in_=z[u][:, a:b])
 
-        chunks = S // CHUNK
-        first(0)
-        for c in range(chunks):
-            if c + 1 < chunks:
-                first(c + 1)
-            quantize_h(c)
-            second(0, c * CHUNK, (c + 1) * CHUNK)
-            if c > 0:
-                scatter(0, (c - 1) * CHUNK, c * CHUNK)
-            if c % 2 == 1:
-                second(1, (c - 1) * CHUNK, (c + 1) * CHUNK)
-        scatter(0, S - CHUNK, S)
+        for c in range(S // CHUNK):
+            first(c)
+        quantize_h(0)
+        second(0, 0, 128, "vector")
+        quantize_h(1)
+        quantize_h(2)
+        scatter(0, 0, 128)
+        quantize_h(3)
+        second(0, 128, 256)
+        light(1, 0)
+        second(0, 256, 512)
+        light(1, 1)
+        scatter(0, 128, 256)
+        scatter(0, 256, 512)
         nc.sync.dma_start(out=out[0:P, :], in_=res[0][:])
-        for h in range(2):
-            scatter(1, h * HALF, (h + 1) * HALF)
+        second(1, 0, 512)
+        scatter(1, 0, 512)
         nc.sync.dma_start(out=out[P : 2 * P, :], in_=res[1][:])

@@ -31,9 +31,10 @@ def tile_moe_cas_mlp_relu_kernel(tc, x_words, x_scales, w_words, w_scales, w1, w
         offsets = keep.tile([P, S // 16], U16, name="offsets")
         xw = [keep.tile([P, T], I32, name="xw%d" % s, align_bytes=64) for s in range(PASSES)]
         xs = keep.tile([P, T], U8, name="xs", align_bytes=64)
-        ww = keep.tile([P, PASSES, N], I32, name="ww", align_bytes=64)
-        ws = keep.tile([P, N], U8, name="ws", align_bytes=64)
-        w1_raw = [[keep.tile([P, PACK, HALF], F32, name="w1_raw%d%d" % (s, h), tag="slab%d%d" % (s, h), align_bytes=64) for h in range(2)] for s in range(PASSES)]
+        ww = [keep.tile([P, PASSES, P], I32, name="ww%d" % u, align_bytes=64) for u in range(2)]
+        ws = keep.tile([P, PASSES, N], U8, name="ws", align_bytes=64)
+        w1_raw0 = keep.tile([P, PACK, H], F32, name="w1_raw0", align_bytes=64)
+        w1_raw1 = [keep.tile([P, PACK, HALF], F32, name="w1_raw1%d" % h, tag="slab1%d" % h, align_bytes=64) for h in range(2)]
         w2_raw = keep.tile([P, PACK, N], F32, name="w2_raw", align_bytes=64)
         w1_bf0 = keep.tile([P, PACK, P, PACK], BF16, name="w1_bf0", align_bytes=64)
         w1_bf1 = [keep.tile([P, PACK, 64, PACK], BF16, name="w1_bf1%d" % h, align_bytes=64) for h in range(2)]
@@ -50,30 +51,32 @@ def tile_moe_cas_mlp_relu_kernel(tc, x_words, x_scales, w_words, w_scales, w1, w
         z = [keep.tile([P, S], F32, name="z%d" % u, align_bytes=64) for u in range(2)]
 
         nc.vector.memset(xs[:].bitcast(I32), 0)
-        nc.vector.memset(ws[:].bitcast(I32), 0)
+        nc.vector.memset(ws[:].rearrange("p s n -> p (s n)").bitcast(I32), 0)
 
         def load_x(s):
             nc.sync.dma_start(out=xw[s][:], in_=x_words[s].rearrange("p t d -> p (t d)").bitcast(I32))
 
-        def load_scales(tile, src):
-            for q in range(4):
-                nc.sync.dma_start(out=tile[32 * q : 32 * q + 8, :].bitcast(I32), in_=src[:, 4 * q : 4 * q + 4, :].bitcast(I32))
+        def load_w(u):
+            words = w_words.rearrange("s p n d -> p s (n d)").bitcast(I32)
+            nc.sync.dma_start(out=ww[u][:], in_=words[:, :, u * P : (u + 1) * P])
 
         w1_rows = w1.rearrange("(s p j) c -> s p j c", s=PASSES, j=PACK)
-        def load_w1(s, h):
-            nc.sync.dma_start(out=w1_raw[s][h][:], in_=w1_rows[s][:, :, h * HALF : (h + 1) * HALF])
-
         load_x(0)
         nc.sync.dma_start(out=offsets[:], in_=offs)
-        load_scales(xs, x_scales)
-        load_w1(0, 0)
+        for q in range(4):
+            nc.sync.dma_start(out=xs[32 * q : 32 * q + 8, :].bitcast(I32), in_=x_scales[:, 4 * q : 4 * q + 4, :].bitcast(I32))
+        nc.sync.dma_start(out=w1_raw0[:], in_=w1_rows[0])
         load_x(1)
-        load_w1(0, 1)
-        load_scales(ws, w_scales)
-        nc.sync.dma_start(out=ww[:], in_=w_words.rearrange("s p n d -> p s (n d)").bitcast(I32))
-        load_w1(1, 0)
-        load_w1(1, 1)
+        for q in range(4):
+            nc.sync.dma_start(
+                out=ws[32 * q : 32 * q + 4, :, :].bitcast(I32),
+                in_=w_scales[:, 4 * q : 4 * q + 4, :].rearrange("s r n -> r s n").bitcast(I32),
+            )
+        load_w(0)
+        for h in range(2):
+            nc.sync.dma_start(out=w1_raw1[h][:], in_=w1_rows[1][:, :, h * HALF : (h + 1) * HALF])
         nc.sync.dma_start(out=w2_raw[:], in_=w2.rearrange("(p j) n -> p j n", j=PACK))
+        load_w(1)
 
         def cast_w1(engine, dst, raw, t0, t1):
             dst = dst[:, t0:t1, :, :].rearrange("p t m j -> p m j t")
@@ -99,8 +102,8 @@ def tile_moe_cas_mlp_relu_kernel(tc, x_words, x_scales, w_words, w_scales, w1, w
                 for s in range(PASSES):
                     nc.tensor.matmul_mx(
                         out=acc[:],
-                        lhsT=ww[:, s, u * P : (u + 1) * P].bitcast(FP8X4),
-                        lhsT_scale=ws[4 * s : P, u * P : (u + 1) * P],
+                        lhsT=ww[u][:, s, :].bitcast(FP8X4),
+                        lhsT_scale=ws[:, s, u * P : (u + 1) * P],
                         rhs=xw[s][:, cols].bitcast(FP8X4),
                         rhs_scale=xs[4 * s : P, cols],
                         start=(s == 0),
@@ -114,18 +117,17 @@ def tile_moe_cas_mlp_relu_kernel(tc, x_words, x_scales, w_words, w_scales, w1, w
 
         nc.vector.tensor_copy(out=gw[0][:], in_=xw[0][:].bitcast(U32).indirect(offsets[:]))
         nc.vector.tensor_copy(out=gs[:], in_=xs[:].indirect(offsets[:]))
-        cast_w1("scalar", w1_bf0[:, :, 0:64, :], w1_raw[0][0], 0, 4)
+        cast_shared(w1_bf0[:], w1_raw0)
         nc.vector.tensor_copy(out=gw[1][:], in_=xw[1][:].bitcast(U32).indirect(offsets[:]))
-        cast_shared(w1_bf0[:, :, 64:128, :], w1_raw[0][1])
         nc.vector.quantize_mx(
             out=w1_codes[0][:].bitcast(FP8X4),
             scales=w1_sc[0][:],
             in_=w1_bf0[:].rearrange("p t m j -> p (t m j)"),
         )
         for h in range(2):
-            cast_shared(w1_bf1[h][:], w1_raw[1][h])
+            cast_shared(w1_bf1[h][:], w1_raw1[h])
             quantize_w1_half(h)
-        res = [keep.tile([P, T], F32, name="res%d" % u, tag=("slab11", "res1")[u], align_bytes=64) for u in range(2)]
+        res = [keep.tile([P, T], F32, name="res%d" % u, tag=("slab10", "res1")[u], align_bytes=64) for u in range(2)]
         light(0, 0)
         light(0, 1)
 
@@ -184,13 +186,16 @@ def tile_moe_cas_mlp_relu_kernel(tc, x_words, x_scales, w_words, w_scales, w1, w
         quantize_h(2)
         scatter(0, 0, 128)
         quantize_h(3)
-        second(0, 128, 256)
         light(1, 0)
-        second(0, 256, 512)
+        second(0, 128, 256)
         light(1, 1)
+        second(1, 0, 128)
+        second(0, 256, 512)
+        second(1, 128, 256)
+        second(1, 256, 512)
         scatter(0, 128, 256)
+        scatter(1, 0, 128)
         scatter(0, 256, 512)
         nc.sync.dma_start(out=out[0:P, :], in_=res[0][:])
-        second(1, 0, 512)
-        scatter(1, 0, 512)
+        scatter(1, 128, 512)
         nc.sync.dma_start(out=out[P : 2 * P, :], in_=res[1][:])

@@ -33,14 +33,13 @@ def tile_moe_cas_mlp_relu_kernel(tc, x_words, x_scales, w_words, w_scales, w1, w
         xs = keep.tile([P, T], U8, name="xs", align_bytes=64)
         ww = [keep.tile([P, PASSES, P], I32, name="ww%d" % u, align_bytes=64) for u in range(2)]
         ws = keep.tile([P, PASSES, N], U8, name="ws", align_bytes=64)
-        w1_raw0 = keep.tile([P, PACK, H], F32, name="w1_raw0", align_bytes=64)
-        w1_raw1 = [keep.tile([P, PACK, HALF], F32, name="w1_raw1%d" % h, tag="slab1%d" % h, align_bytes=64) for h in range(2)]
+        w1_raw = [keep.tile([P, PACK, H], F32, name="w1_raw%d" % s, align_bytes=64) for s in range(PASSES)]
         w2_raw = keep.tile([P, PACK, N], F32, name="w2_raw", align_bytes=64)
-        w1_bf0 = keep.tile([P, PACK, P, PACK], BF16, name="w1_bf0", align_bytes=64)
-        w1_bf1 = [keep.tile([P, PACK, 64, PACK], BF16, name="w1_bf1%d" % h, align_bytes=64) for h in range(2)]
+        w1_bf = [keep.tile([P, PACK, P, PACK], BF16, name="w1_bf%d" % s, align_bytes=64) for s in range(PASSES)]
+        res = [keep.tile([P, T], F32, name="res%d" % u, align_bytes=64) for u in range(2)]
         w1_codes = [keep.tile([P, H], U32, name="w1_codes%d" % s, align_bytes=64) for s in range(PASSES)]
         w1_sc = [keep.tile([P, H], U8, name="w1_sc%d" % s, align_bytes=64) for s in range(PASSES)]
-        w2_bf = keep.tile([P, N, PACK], BF16, name="w2_bf", align_bytes=64)
+        w2_bf = [keep.tile([P, P, PACK], BF16, name="w2_bf%d" % u, align_bytes=64) for u in range(2)]
         w2_codes = keep.tile([P, N], U32, name="w2_codes", align_bytes=64)
         w2_sc = keep.tile([P, N], U8, name="w2_sc", align_bytes=64)
         gw = [keep.tile([P, S], U32, name="gw%d" % s, align_bytes=64) for s in range(PASSES)]
@@ -65,16 +64,15 @@ def tile_moe_cas_mlp_relu_kernel(tc, x_words, x_scales, w_words, w_scales, w1, w
         nc.sync.dma_start(out=offsets[:], in_=offs)
         for q in range(4):
             nc.sync.dma_start(out=xs[32 * q : 32 * q + 8, :].bitcast(I32), in_=x_scales[:, 4 * q : 4 * q + 4, :].bitcast(I32))
-        nc.sync.dma_start(out=w1_raw0[:], in_=w1_rows[0])
-        load_x(1)
+        nc.sync.dma_start(out=w1_raw[0][:], in_=w1_rows[0])
         for q in range(4):
             nc.sync.dma_start(
                 out=ws[32 * q : 32 * q + 4, :, :].bitcast(I32),
                 in_=w_scales[:, 4 * q : 4 * q + 4, :].rearrange("s r n -> r s n").bitcast(I32),
             )
         load_w(0)
-        for h in range(2):
-            nc.sync.dma_start(out=w1_raw1[h][:], in_=w1_rows[1][:, :, h * HALF : (h + 1) * HALF])
+        nc.sync.dma_start(out=w1_raw[1][:], in_=w1_rows[1])
+        load_x(1)
         nc.sync.dma_start(out=w2_raw[:], in_=w2.rearrange("(p j) n -> p j n", j=PACK))
         load_w(1)
 
@@ -86,30 +84,37 @@ def tile_moe_cas_mlp_relu_kernel(tc, x_words, x_scales, w_words, w_scales, w1, w
             else:
                 nc.vector.tensor_copy(out=dst, in_=src)
 
-        def quantize_w1_half(h):
-            for t in range(PACK):
-                cols = slice(t * P + h * 64, t * P + (h + 1) * 64)
-                nc.vector.quantize_mx(
-                    out=w1_codes[1][:, cols].bitcast(FP8X4),
-                    scales=w1_sc[1][:, cols],
-                    in_=w1_bf1[h][:, t, :, :].rearrange("p m j -> p (m j)"),
-                )
+        def quantize_w1(s, t0, t1):
+            cols = slice(t0 * P, t1 * P)
+            nc.vector.quantize_mx(
+                out=w1_codes[s][:, cols].bitcast(FP8X4),
+                scales=w1_sc[s][:, cols],
+                in_=w1_bf[s][:, t0:t1, :, :].rearrange("p t m j -> p (t m j)"),
+            )
+
+        def light_pass(acc, u, g, s):
+            cols = slice(g * 512, (g + 1) * 512)
+            nc.tensor.matmul_mx(
+                out=acc[:],
+                lhsT=ww[u][:, s, :].bitcast(FP8X4),
+                lhsT_scale=ws[:, s, u * P : (u + 1) * P],
+                rhs=xw[s][:, cols].bitcast(FP8X4),
+                rhs_scale=xs[4 * s : P, cols],
+                start=(s == 0),
+                stop=(s == PASSES - 1),
+            )
+
+        def light_open(u, g):
+            acc = psum.tile([P, 512], F32, name="acc")
+            light_pass(acc, u, g, 0)
+            return acc
+
+        def light_close(acc, u, g):
+            light_pass(acc, u, g, 1)
+            nc.scalar.activation(out=res[u][:, g * 512 : (g + 1) * 512], in_=acc[:], func=COPY)
 
         def light(u, g):
-            if True:
-                acc = psum.tile([P, 512], F32, name="acc")
-                cols = slice(g * 512, (g + 1) * 512)
-                for s in range(PASSES):
-                    nc.tensor.matmul_mx(
-                        out=acc[:],
-                        lhsT=ww[u][:, s, :].bitcast(FP8X4),
-                        lhsT_scale=ws[:, s, u * P : (u + 1) * P],
-                        rhs=xw[s][:, cols].bitcast(FP8X4),
-                        rhs_scale=xs[4 * s : P, cols],
-                        start=(s == 0),
-                        stop=(s == PASSES - 1),
-                    )
-                nc.scalar.activation(out=res[u][:, cols], in_=acc[:], func=COPY)
+            light_close(light_open(u, g), u, g)
 
         def cast_shared(dst, raw):
             cast_w1("vector", dst, raw, 0, 2)
@@ -117,25 +122,25 @@ def tile_moe_cas_mlp_relu_kernel(tc, x_words, x_scales, w_words, w_scales, w1, w
 
         nc.vector.tensor_copy(out=gw[0][:], in_=xw[0][:].bitcast(U32).indirect(offsets[:]))
         nc.vector.tensor_copy(out=gs[:], in_=xs[:].indirect(offsets[:]))
-        cast_shared(w1_bf0[:], w1_raw0)
-        nc.vector.tensor_copy(out=gw[1][:], in_=xw[1][:].bitcast(U32).indirect(offsets[:]))
-        nc.vector.quantize_mx(
-            out=w1_codes[0][:].bitcast(FP8X4),
-            scales=w1_sc[0][:],
-            in_=w1_bf0[:].rearrange("p t m j -> p (t m j)"),
-        )
-        for h in range(2):
-            cast_shared(w1_bf1[h][:], w1_raw1[h])
-            quantize_w1_half(h)
-        res = [keep.tile([P, T], F32, name="res%d" % u, tag=("slab10", "res1")[u], align_bytes=64) for u in range(2)]
-        light(0, 0)
-        light(0, 1)
+        cast_shared(w1_bf[0][:], w1_raw[0])
+        quantize_w1(0, 0, 4)
+        cast_shared(w1_bf[1][:], w1_raw[1])
+        quantize_w1(1, 0, 2)
+        quantize_w1(1, 2, 4)
+        opened = [light_open(0, g) for g in range(2)]
+        for a, b in ((0, 128), (128, 256), (256, 512)):
+            nc.vector.tensor_copy(out=gw[1][:, a:b], in_=xw[1][:].bitcast(U32).indirect(offsets[:, a // 16 : b // 16]))
+        for g in range(2):
+            light_close(opened[g], 0, g)
 
-        nc.vector.tensor_copy(
-            out=w2_bf[:].rearrange("p (c i) j -> p c j i", i=PACK),
-            in_=w2_raw[:].rearrange("p j (c i) -> p c j i", i=PACK),
-        )
-        nc.vector.quantize_mx(out=w2_codes[:].bitcast(FP8X4), scales=w2_sc[:], in_=w2_bf[:].rearrange("p n j -> p (n j)"))
+        for u in range(2):
+            nc.vector.tensor_copy(
+                out=w2_bf[u][:].rearrange("p (c i) j -> p c j i", i=PACK),
+                in_=w2_raw[:, :, u * P : (u + 1) * P].rearrange("p j (c i) -> p c j i", i=PACK),
+            )
+        for u in range(2):
+            cols = slice(u * P, (u + 1) * P)
+            nc.vector.quantize_mx(out=w2_codes[:, cols].bitcast(FP8X4), scales=w2_sc[:, cols], in_=w2_bf[u][:].rearrange("p n j -> p (n j)"))
 
         def first(c):
             slots = slice(c * CHUNK, (c + 1) * CHUNK)

@@ -62,9 +62,17 @@ def tile_moe_cas_mlp_relu_kernel(tc, x_words, x_scales, w_words, w_scales, w1, w
         w1_rows = w1.rearrange("(s p j) c -> s p j c", s=PASSES, j=PACK)
         load_x(0)
         nc.sync.dma_start(out=offsets[:], in_=offs)
-        for q in range(4):
+        def load_x_scales(q, s):
+            row = 32 * q + 4 * s
+            nc.sync.dma_start(out=xs[row : row + 4, :].bitcast(I32), in_=x_scales[s, 4 * q : 4 * q + 4, :].bitcast(I32))
+
+        for q in range(2):
             nc.sync.dma_start(out=xs[32 * q : 32 * q + 8, :].bitcast(I32), in_=x_scales[:, 4 * q : 4 * q + 4, :].bitcast(I32))
+        load_x_scales(2, 0)
+        load_x_scales(2, 1)
+        load_x_scales(3, 0)
         nc.sync.dma_start(out=w1_raw[0][:], in_=w1_rows[0])
+        load_x_scales(3, 1)
         for q in range(4):
             nc.sync.dma_start(
                 out=ws[32 * q : 32 * q + 4, :, :].bitcast(I32),

@@ -136,6 +136,17 @@ def tile_moe_cas_mlp_relu_kernel(tc, x_words, x_scales, w_words, w_scales, w1, w
         quantize_w1(1, 0, 2)
         quantize_w1(1, 2, 4)
         opened = [light_open(0, g) for g in range(2)]
+        warm = psum.tile([P, 512], F32, name="acc")
+        for a, b in ((0, 512), (0, 256), (256, 384)):
+            nc.tensor.matmul_mx(
+                out=warm[:, a:b],
+                lhsT=w1_codes[0][:, 0:P].bitcast(FP8X4),
+                lhsT_scale=w1_sc[0][:, 0:P],
+                rhs=gw[0][:, a:b].bitcast(FP8X4),
+                rhs_scale=gs[:, a:b],
+                start=True,
+                stop=True,
+            )
         for a, b in ((0, 128), (128, 256), (256, 512)):
             nc.vector.tensor_copy(out=gw[1][:, a:b], in_=xw[1][:].bitcast(U32).indirect(offsets[:, a // 16 : b // 16]))
         for g in range(2):

@@ -34,7 +34,7 @@ def tile_moe_cas_mlp_relu_kernel(tc, x_words, x_scales, w_words, w_scales, w1, w
         ww = [keep.tile([P, PASSES, P], I32, name="ww%d" % u, align_bytes=64) for u in range(2)]
         ws = keep.tile([P, PASSES, N], U8, name="ws", align_bytes=64)
         w1_raw = [keep.tile([P, PACK, H], F32, name="w1_raw%d" % s, align_bytes=64) for s in range(PASSES)]
-        w2_raw = keep.tile([P, PACK, N], F32, name="w2_raw", align_bytes=64)
+        w2_raw = [keep.tile([P, PACK, P], F32, name="w2_raw%d" % u, align_bytes=64) for u in range(2)]
         w1_bf = [keep.tile([P, PACK, P, PACK], BF16, name="w1_bf%d" % s, align_bytes=64) for s in range(PASSES)]
         res = [keep.tile([P, T], F32, name="res%d" % u, align_bytes=64) for u in range(2)]
         w1_codes = [keep.tile([P, H], U32, name="w1_codes%d" % s, align_bytes=64) for s in range(PASSES)]
@@ -60,29 +60,46 @@ def tile_moe_cas_mlp_relu_kernel(tc, x_words, x_scales, w_words, w_scales, w1, w
             nc.sync.dma_start(out=ww[u][:], in_=words[:, :, u * P : (u + 1) * P])
 
         w1_rows = w1.rearrange("(s p j) c -> s p j c", s=PASSES, j=PACK)
-        load_x(0)
-        nc.sync.dma_start(out=offsets[:], in_=offs)
+        w2_rows = w2.rearrange("(p j) n -> p j n", j=PACK)
+
         def load_x_scales(q, s):
             row = 32 * q + 4 * s
             nc.sync.dma_start(out=xs[row : row + 4, :].bitcast(I32), in_=x_scales[s, 4 * q : 4 * q + 4, :].bitcast(I32))
 
-        for q in range(2):
+        def load_x_scales_both(q):
             nc.sync.dma_start(out=xs[32 * q : 32 * q + 8, :].bitcast(I32), in_=x_scales[:, 4 * q : 4 * q + 4, :].bitcast(I32))
+
+        def load_w_scales():
+            for q in range(4):
+                nc.sync.dma_start(
+                    out=ws[32 * q : 32 * q + 4, :, :].bitcast(I32),
+                    in_=w_scales[:, 4 * q : 4 * q + 4, :].rearrange("s r n -> r s n").bitcast(I32),
+                )
+
+        def load_w1(s):
+            nc.sync.dma_start(out=w1_raw[s][:], in_=w1_rows[s])
+
+        def load_w2(u):
+            nc.sync.dma_start(out=w2_raw[u][:], in_=w2_rows[:, :, u * P : (u + 1) * P])
+
+        load_x(0)
+        nc.sync.dma_start(out=offsets[:], in_=offs)
+        for q in range(2):
+            load_x_scales_both(q)
         load_x_scales(2, 0)
         load_x_scales(2, 1)
         load_x_scales(3, 0)
-        nc.sync.dma_start(out=w1_raw[0][:], in_=w1_rows[0])
+        load_w1(0)
         load_x_scales(3, 1)
-        for q in range(4):
-            nc.sync.dma_start(
-                out=ws[32 * q : 32 * q + 4, :, :].bitcast(I32),
-                in_=w_scales[:, 4 * q : 4 * q + 4, :].rearrange("s r n -> r s n").bitcast(I32),
-            )
+        load_w_scales()
         load_w(0)
-        nc.sync.dma_start(out=w1_raw[1][:], in_=w1_rows[1])
-        load_x(1)
-        nc.sync.dma_start(out=w2_raw[:], in_=w2.rearrange("(p j) n -> p j n", j=PACK))
+        load_w1(1)
+        for g in range(2):
+            words = x_words[1].rearrange("p t d -> p (t d)").bitcast(I32)
+            nc.sync.dma_start(out=xw[1][:, g * 512 : (g + 1) * 512], in_=words[:, g * 512 : (g + 1) * 512])
+        load_w2(0)
         load_w(1)
+        load_w2(1)
 
         def cast_w1(engine, dst, raw, t0, t1):
             dst = dst[:, t0:t1, :, :].rearrange("p t m j -> p m j t")
@@ -121,9 +138,6 @@ def tile_moe_cas_mlp_relu_kernel(tc, x_words, x_scales, w_words, w_scales, w1, w
             light_pass(acc, u, g, 1)
             nc.scalar.activation(out=res[u][:, g * 512 : (g + 1) * 512], in_=acc[:], func=COPY)
 
-        def light(u, g):
-            light_close(light_open(u, g), u, g)
-
         def cast_shared(dst, raw):
             cast_w1("vector", dst, raw, 0, 2)
             cast_w1("scalar", dst, raw, 2, 4)
@@ -131,51 +145,57 @@ def tile_moe_cas_mlp_relu_kernel(tc, x_words, x_scales, w_words, w_scales, w1, w
         nc.vector.tensor_copy(out=gw[0][:], in_=xw[0][:].bitcast(U32).indirect(offsets[:]))
         nc.vector.tensor_copy(out=gs[:], in_=xs[:].indirect(offsets[:]))
         cast_shared(w1_bf[0][:], w1_raw[0])
-        quantize_w1(0, 0, 4)
+        quantize_w1(0, 0, 2)
+        quantize_w1(0, 2, 4)
         cast_shared(w1_bf[1][:], w1_raw[1])
         quantize_w1(1, 0, 2)
         quantize_w1(1, 2, 4)
         opened = [light_open(0, g) for g in range(2)]
-        warm = psum.tile([P, 512], F32, name="acc")
-        for a, b in ((0, 512), (0, 256), (256, 384)):
-            nc.tensor.matmul_mx(
-                out=warm[:, a:b],
-                lhsT=w1_codes[0][:, 0:P].bitcast(FP8X4),
-                lhsT_scale=w1_sc[0][:, 0:P],
-                rhs=gw[0][:, a:b].bitcast(FP8X4),
-                rhs_scale=gs[:, a:b],
-                start=True,
-                stop=True,
-            )
-        for a, b in ((0, 128), (128, 256), (256, 512)):
-            nc.vector.tensor_copy(out=gw[1][:, a:b], in_=xw[1][:].bitcast(U32).indirect(offsets[:, a // 16 : b // 16]))
-        for g in range(2):
-            light_close(opened[g], 0, g)
 
-        for u in range(2):
-            nc.vector.tensor_copy(
-                out=w2_bf[u][:].rearrange("p (c i) j -> p c j i", i=PACK),
-                in_=w2_raw[:, :, u * P : (u + 1) * P].rearrange("p j (c i) -> p c j i", i=PACK),
-            )
-        for u in range(2):
-            cols = slice(u * P, (u + 1) * P)
-            nc.vector.quantize_mx(out=w2_codes[:, cols].bitcast(FP8X4), scales=w2_sc[:, cols], in_=w2_bf[u][:].rearrange("p n j -> p (n j)"))
-
-        def first(c):
+        def first_pass(acc, c, t, s, start, stop):
             slots = slice(c * CHUNK, (c + 1) * CHUNK)
+            nc.tensor.matmul_mx(
+                out=acc[:, t, :],
+                lhsT=w1_codes[s][:, t * P : (t + 1) * P].bitcast(FP8X4),
+                lhsT_scale=w1_sc[s][:, t * P : (t + 1) * P],
+                rhs=gw[s][:, slots].bitcast(FP8X4),
+                rhs_scale=gs[4 * s : P, slots],
+                start=start,
+                stop=stop,
+            )
+
+        def first_open(c):
             acc = psum.tile([P, PACK, CHUNK], F32, name="acc")
             for t in range(PACK):
-                for s in range(PASSES):
-                    nc.tensor.matmul_mx(
-                        out=acc[:, t, :],
-                        lhsT=w1_codes[s][:, t * P : (t + 1) * P].bitcast(FP8X4),
-                        lhsT_scale=w1_sc[s][:, t * P : (t + 1) * P],
-                        rhs=gw[s][:, slots].bitcast(FP8X4),
-                        rhs_scale=gs[4 * s : P, slots],
-                        start=(s == 0),
-                        stop=(s == PASSES - 1),
-                    )
+                first_pass(acc, c, t, 0, t == 0, False)
+            return acc
+
+        def relu(acc, c):
             nc.scalar.activation(out=h_bf[c][:], in_=acc[:].rearrange("p t n -> p n t"), func=RELU)
+
+        def first_close(acc, c):
+            for t in range(PACK):
+                first_pass(acc, c, t, 1, False, t == PACK - 1)
+            relu(acc, c)
+
+        def first(c):
+            acc = psum.tile([P, PACK, CHUNK], F32, name="acc")
+            for t in range(PACK):
+                for s in (1, 0):
+                    first_pass(acc, c, t, s, s == 1, s == 0)
+            relu(acc, c)
+
+        def cast_w2(engine, u):
+            dst = w2_bf[u][:].rearrange("p (c i) j -> p c j i", i=PACK)
+            src = w2_raw[u][:].rearrange("p j (c i) -> p c j i", i=PACK)
+            if engine == "scalar":
+                nc.scalar.activation(out=dst, in_=src, func=COPY)
+            else:
+                nc.vector.tensor_copy(out=dst, in_=src)
+
+        def quantize_w2(u):
+            cols = slice(u * P, (u + 1) * P)
+            nc.vector.quantize_mx(out=w2_codes[:, cols].bitcast(FP8X4), scales=w2_sc[:, cols], in_=w2_bf[u][:].rearrange("p n j -> p (n j)"))
 
         def quantize_h(c):
             slots = slice(c * CHUNK, (c + 1) * CHUNK)
@@ -183,7 +203,7 @@ def tile_moe_cas_mlp_relu_kernel(tc, x_words, x_scales, w_words, w_scales, w1, w
                 out=h_codes[:, slots].bitcast(FP8X4), scales=h_sc[:, slots], in_=h_bf[c][:].rearrange("p n t -> p (n t)")
             )
 
-        def second(u, a, b, engine="scalar"):
+        def second(u, a, b):
             acc = psum.tile([P, b - a], F32, name="acc")
             nc.tensor.matmul_mx(
                 out=acc[:],
@@ -194,32 +214,56 @@ def tile_moe_cas_mlp_relu_kernel(tc, x_words, x_scales, w_words, w_scales, w1, w
                 start=True,
                 stop=True,
             )
+            return acc
+
+        def copy_z(acc, u, a, b, engine="scalar"):
             if engine == "scalar":
                 nc.scalar.activation(out=z[u][:, a:b], in_=acc[:], func=COPY)
             else:
                 nc.vector.tensor_copy(out=z[u][:, a:b], in_=acc[:])
 
+        def light_products(u, g):
+            acc = light_open(u, g)
+            light_pass(acc, u, g, 1)
+            return acc
+
+        def light_copy(acc, u, g):
+            nc.scalar.activation(out=res[u][:, g * 512 : (g + 1) * 512], in_=acc[:], func=COPY)
+
         def scatter(u, a, b):
             nc.vector.tensor_copy(out=res[u][:].indirect(offsets[:, a // 16 : b // 16]), in_=z[u][:, a:b])
 
-        for c in range(S // CHUNK):
-            first(c)
+        early = [first_open(c) for c in range(2)]
+        for a, b in ((0, 128), (128, 256), (256, 384), (384, 512)):
+            nc.vector.tensor_copy(out=gw[1][:, a:b], in_=xw[1][:].bitcast(U32).indirect(offsets[:, a // 16 : b // 16]))
+        light_close(opened[0], 0, 0)
+        first_close(early[0], 0)
+        light_close(opened[1], 0, 1)
+        first_close(early[1], 1)
+        cast_w2("vector", 0)
+        quantize_w2(0)
+        first(2)
+        first(3)
         quantize_h(0)
-        second(0, 0, 128, "vector")
+        copy_z(second(0, 0, 128), 0, 0, 128, "vector")
         quantize_h(1)
+        cast_w2("vector", 1)
+        quantize_w2(1)
         quantize_h(2)
         scatter(0, 0, 128)
         quantize_h(3)
-        light(1, 0)
-        second(0, 128, 256)
-        light(1, 1)
-        second(1, 0, 128)
-        second(0, 256, 512)
-        second(1, 128, 256)
-        second(1, 256, 512)
+        late = [light_products(1, 0)]
+        copy_z(second(0, 128, 256), 0, 128, 256)
+        late.append(light_products(1, 1))
         scatter(0, 128, 256)
+        for g in range(2):
+            light_copy(late[g], 1, g)
+        copy_z(second(1, 0, 128), 1, 0, 128)
         scatter(1, 0, 128)
+        copy_z(second(0, 256, 512), 0, 256, 512)
         scatter(0, 256, 512)
         nc.sync.dma_start(out=out[0:P, :], in_=res[0][:])
+        copy_z(second(1, 128, 256), 1, 128, 256)
+        copy_z(second(1, 256, 512), 1, 256, 512)
         scatter(1, 128, 512)
         nc.sync.dma_start(out=out[P : 2 * P, :], in_=res[1][:])

@@ -19,19 +19,21 @@ P = 128
 PACK = 4
 PASSES = 2
 CHUNK = 128
-HALF = 256
+SHARE = 32
+NE = 3
 
 
 def tile_moe_cas_mlp_relu_kernel(tc, x_words, x_scales, w_words, w_scales, w1, w2, offs, out):
     nc = tc.nc
     with ExitStack() as ctx:
         keep = ctx.enter_context(tc.tile_pool(name="keep", bufs=1))
-        psum = ctx.enter_context(tc.psum_pool(name="psum", bufs=8))
+        psum = ctx.enter_context(tc.psum_pool(name="psum", bufs=7))
 
         offsets = keep.tile([P, S // 16], U16, name="offsets")
         xw = [keep.tile([P, T], I32, name="xw%d" % s, align_bytes=64) for s in range(PASSES)]
         xs = keep.tile([P, T], U8, name="xs", align_bytes=64)
-        ww = [keep.tile([P, PASSES, P], I32, name="ww%d" % u, align_bytes=64) for u in range(2)]
+        ww0 = [keep.tile([P, P], I32, name="ww0%d" % s, align_bytes=64) for s in range(PASSES)]
+        ww1 = keep.tile([P, PASSES, P], I32, name="ww1", align_bytes=64)
         ws = keep.tile([P, PASSES, N], U8, name="ws", align_bytes=64)
         w1_raw = [keep.tile([P, PACK, H], F32, name="w1_raw%d" % s, align_bytes=64) for s in range(PASSES)]
         w2_raw = [keep.tile([P, PACK, P], F32, name="w2_raw%d" % u, align_bytes=64) for u in range(2)]
@@ -42,7 +44,8 @@ def tile_moe_cas_mlp_relu_kernel(tc, x_words, x_scales, w_words, w_scales, w1, w
         w2_bf = [keep.tile([P, P, PACK], BF16, name="w2_bf%d" % u, align_bytes=64) for u in range(2)]
         w2_codes = keep.tile([P, N], U32, name="w2_codes", align_bytes=64)
         w2_sc = keep.tile([P, N], U8, name="w2_sc", align_bytes=64)
-        gw = [keep.tile([P, S], U32, name="gw%d" % s, align_bytes=64) for s in range(PASSES)]
+        gw0 = keep.tile([P, S], U32, name="gw0", align_bytes=64)
+        gw1 = []
         gs = keep.tile([P, S], U8, name="gs", align_bytes=64)
         h_bf = [keep.tile([P, CHUNK, PACK], BF16, name="h_bf%d" % c, align_bytes=64) for c in range(S // CHUNK)]
         h_codes = keep.tile([P, S], U32, name="h_codes", align_bytes=64)
@@ -55,9 +58,13 @@ def tile_moe_cas_mlp_relu_kernel(tc, x_words, x_scales, w_words, w_scales, w1, w
         def load_x(s):
             nc.sync.dma_start(out=xw[s][:], in_=x_words[s].rearrange("p t d -> p (t d)").bitcast(I32))
 
-        def load_w(u):
-            words = w_words.rearrange("s p n d -> p s (n d)").bitcast(I32)
-            nc.sync.dma_start(out=ww[u][:], in_=words[:, :, u * P : (u + 1) * P])
+        words_w = w_words.rearrange("s p n d -> p s (n d)").bitcast(I32)
+
+        def load_w0(s):
+            nc.sync.dma_start(out=ww0[s][:], in_=words_w[:, s, 0:P])
+
+        def load_w_late():
+            nc.sync.dma_start(out=ww1[:], in_=words_w[:, :, P : 2 * P])
 
         w1_rows = w1.rearrange("(s p j) c -> s p j c", s=PASSES, j=PACK)
         w2_rows = w2.rearrange("(p j) n -> p j n", j=PACK)
@@ -92,18 +99,19 @@ def tile_moe_cas_mlp_relu_kernel(tc, x_words, x_scales, w_words, w_scales, w1, w
         load_w1(0)
         load_x_scales(3, 1)
         load_w_scales()
-        load_w(0)
+        load_w0(0)
         load_w1(1)
+        load_w0(1)
         for g in range(2):
             words = x_words[1].rearrange("p t d -> p (t d)").bitcast(I32)
             nc.sync.dma_start(out=xw[1][:, g * 512 : (g + 1) * 512], in_=words[:, g * 512 : (g + 1) * 512])
         load_w2(0)
-        load_w(1)
+        load_w_late()
         load_w2(1)
 
-        def cast_w1(engine, dst, raw, t0, t1):
-            dst = dst[:, t0:t1, :, :].rearrange("p t m j -> p m j t")
-            src = raw[:].rearrange("p j (m t) -> p m j t", t=PACK)[:, :, :, t0:t1]
+        def cast_w1(engine, dst, raw, t0, t1, m0=0, m1=P):
+            dst = dst[:, t0:t1, m0:m1, :].rearrange("p t m j -> p m j t")
+            src = raw[:].rearrange("p j (m t) -> p m j t", t=PACK)[:, m0:m1, :, t0:t1]
             if engine == "scalar":
                 nc.scalar.activation(out=dst, in_=src, func=COPY)
             else:
@@ -121,7 +129,7 @@ def tile_moe_cas_mlp_relu_kernel(tc, x_words, x_scales, w_words, w_scales, w1, w
             cols = slice(g * 512, (g + 1) * 512)
             nc.tensor.matmul_mx(
                 out=acc[:],
-                lhsT=ww[u][:, s, :].bitcast(FP8X4),
+                lhsT=(ww0[s][:] if u == 0 else ww1[:, s, :]).bitcast(FP8X4),
                 lhsT_scale=ws[:, s, u * P : (u + 1) * P],
                 rhs=xw[s][:, cols].bitcast(FP8X4),
                 rhs_scale=xs[4 * s : P, cols],
@@ -130,7 +138,10 @@ def tile_moe_cas_mlp_relu_kernel(tc, x_words, x_scales, w_words, w_scales, w1, w
             )
 
         def light_open(u, g):
-            acc = psum.tile([P, 512], F32, name="acc")
+            if u == 0 and g == 0:
+                acc = psum.tile([P, 512], F32, name="shared", bufs=1)
+            else:
+                acc = psum.tile([P, 512], F32, name="acc")
             light_pass(acc, u, g, 0)
             return acc
 
@@ -142,12 +153,14 @@ def tile_moe_cas_mlp_relu_kernel(tc, x_words, x_scales, w_words, w_scales, w1, w
             cast_w1("vector", dst, raw, 0, 2)
             cast_w1("scalar", dst, raw, 2, 4)
 
-        nc.vector.tensor_copy(out=gw[0][:], in_=xw[0][:].bitcast(U32).indirect(offsets[:]))
+        nc.vector.tensor_copy(out=gw0[:], in_=xw[0][:].bitcast(U32).indirect(offsets[:]))
         nc.vector.tensor_copy(out=gs[:], in_=xs[:].indirect(offsets[:]))
         cast_shared(w1_bf[0][:], w1_raw[0])
         quantize_w1(0, 0, 2)
         quantize_w1(0, 2, 4)
-        cast_shared(w1_bf[1][:], w1_raw[1])
+        cast_w1("vector", w1_bf[1][:], w1_raw[1], 0, 2)
+        cast_w1("scalar", w1_bf[1][:], w1_raw[1], 2, 4, SHARE, P)
+        cast_w1("vector", w1_bf[1][:], w1_raw[1], 2, 4, 0, SHARE)
         quantize_w1(1, 0, 2)
         quantize_w1(1, 2, 4)
         opened = [light_open(0, g) for g in range(2)]
@@ -158,14 +171,17 @@ def tile_moe_cas_mlp_relu_kernel(tc, x_words, x_scales, w_words, w_scales, w1, w
                 out=acc[:, t, :],
                 lhsT=w1_codes[s][:, t * P : (t + 1) * P].bitcast(FP8X4),
                 lhsT_scale=w1_sc[s][:, t * P : (t + 1) * P],
-                rhs=gw[s][:, slots].bitcast(FP8X4),
+                rhs=(gw0[:, slots] if s == 0 else gw1[c][:]).bitcast(FP8X4),
                 rhs_scale=gs[4 * s : P, slots],
                 start=start,
                 stop=stop,
             )
 
         def first_open(c):
-            acc = psum.tile([P, PACK, CHUNK], F32, name="acc")
+            if c == 3:
+                acc = psum.tile([P, PACK, CHUNK], F32, name="shared", bufs=1)
+            else:
+                acc = psum.tile([P, PACK, CHUNK], F32, name="acc")
             for t in range(PACK):
                 first_pass(acc, c, t, 0, t == 0, False)
             return acc
@@ -233,17 +249,25 @@ def tile_moe_cas_mlp_relu_kernel(tc, x_words, x_scales, w_words, w_scales, w1, w
         def scatter(u, a, b):
             nc.vector.tensor_copy(out=res[u][:].indirect(offsets[:, a // 16 : b // 16]), in_=z[u][:, a:b])
 
-        early = [first_open(c) for c in range(2)]
-        for a, b in ((0, 128), (128, 256), (256, 384), (384, 512)):
-            nc.vector.tensor_copy(out=gw[1][:, a:b], in_=xw[1][:].bitcast(U32).indirect(offsets[:, a // 16 : b // 16]))
+        def gather_late(c):
+            piece = keep.tile([P, CHUNK], U32, name="gw1", bufs=3, align_bytes=64)
+            gw1.append(piece)
+            cols = slice(c * CHUNK // 16, (c + 1) * CHUNK // 16)
+            nc.vector.tensor_copy(out=piece[:], in_=xw[1][:].bitcast(U32).indirect(offsets[:, cols]))
+
+        early = [first_open(c) for c in range(NE)]
+        for c in range(3):
+            gather_late(c)
         light_close(opened[0], 0, 0)
         first_close(early[0], 0)
+        early.append(first_open(3))
         light_close(opened[1], 0, 1)
         first_close(early[1], 1)
         cast_w2("vector", 0)
+        gather_late(3)
         quantize_w2(0)
-        first(2)
-        first(3)
+        for c in range(2, 4):
+            first_close(early[c], c)
         quantize_h(0)
         copy_z(second(0, 0, 128), 0, 0, 128, "vector")
         quantize_h(1)

@@ -20,14 +20,14 @@ PACK = 4
 PASSES = 2
 CHUNK = 128
 SHARE = 32
-NE = 3
+HALF = 256
 
 
 def tile_moe_cas_mlp_relu_kernel(tc, x_words, x_scales, w_words, w_scales, w1, w2, offs, out):
     nc = tc.nc
     with ExitStack() as ctx:
         keep = ctx.enter_context(tc.tile_pool(name="keep", bufs=1))
-        psum = ctx.enter_context(tc.psum_pool(name="psum", bufs=7))
+        psum = ctx.enter_context(tc.psum_pool(name="psum", bufs=8))
 
         offsets = keep.tile([P, S // 16], U16, name="offsets")
         xw = [keep.tile([P, T], I32, name="xw%d" % s, align_bytes=64) for s in range(PASSES)]
@@ -44,8 +44,7 @@ def tile_moe_cas_mlp_relu_kernel(tc, x_words, x_scales, w_words, w_scales, w1, w
         w2_bf = [keep.tile([P, P, PACK], BF16, name="w2_bf%d" % u, align_bytes=64) for u in range(2)]
         w2_codes = keep.tile([P, N], U32, name="w2_codes", align_bytes=64)
         w2_sc = keep.tile([P, N], U8, name="w2_sc", align_bytes=64)
-        gw0 = keep.tile([P, S], U32, name="gw0", align_bytes=64)
-        gw1 = []
+        gw = [keep.tile([P, S], U32, name="gw%d" % s, align_bytes=64) for s in range(PASSES)]
         gs = keep.tile([P, S], U8, name="gs", align_bytes=64)
         h_bf = [keep.tile([P, CHUNK, PACK], BF16, name="h_bf%d" % c, align_bytes=64) for c in range(S // CHUNK)]
         h_codes = keep.tile([P, S], U32, name="h_codes", align_bytes=64)
@@ -138,10 +137,7 @@ def tile_moe_cas_mlp_relu_kernel(tc, x_words, x_scales, w_words, w_scales, w1, w
             )
 
         def light_open(u, g):
-            if u == 0 and g == 0:
-                acc = psum.tile([P, 512], F32, name="shared", bufs=1)
-            else:
-                acc = psum.tile([P, 512], F32, name="acc")
+            acc = psum.tile([P, 512], F32, name="acc")
             light_pass(acc, u, g, 0)
             return acc
 
@@ -153,7 +149,7 @@ def tile_moe_cas_mlp_relu_kernel(tc, x_words, x_scales, w_words, w_scales, w1, w
             cast_w1("vector", dst, raw, 0, 2)
             cast_w1("scalar", dst, raw, 2, 4)
 
-        nc.vector.tensor_copy(out=gw0[:], in_=xw[0][:].bitcast(U32).indirect(offsets[:]))
+        nc.vector.tensor_copy(out=gw[0][:], in_=xw[0][:].bitcast(U32).indirect(offsets[:]))
         nc.vector.tensor_copy(out=gs[:], in_=xs[:].indirect(offsets[:]))
         cast_shared(w1_bf[0][:], w1_raw[0])
         quantize_w1(0, 0, 2)
@@ -171,17 +167,14 @@ def tile_moe_cas_mlp_relu_kernel(tc, x_words, x_scales, w_words, w_scales, w1, w
                 out=acc[:, t, :],
                 lhsT=w1_codes[s][:, t * P : (t + 1) * P].bitcast(FP8X4),
                 lhsT_scale=w1_sc[s][:, t * P : (t + 1) * P],
-                rhs=(gw0[:, slots] if s == 0 else gw1[c][:]).bitcast(FP8X4),
+                rhs=gw[s][:, slots].bitcast(FP8X4),
                 rhs_scale=gs[4 * s : P, slots],
                 start=start,
                 stop=stop,
             )
 
         def first_open(c):
-            if c == 3:
-                acc = psum.tile([P, PACK, CHUNK], F32, name="shared", bufs=1)
-            else:
-                acc = psum.tile([P, PACK, CHUNK], F32, name="acc")
+            acc = psum.tile([P, PACK, CHUNK], F32, name="acc")
             for t in range(PACK):
                 first_pass(acc, c, t, 0, t == 0, False)
             return acc
@@ -249,25 +242,17 @@ def tile_moe_cas_mlp_relu_kernel(tc, x_words, x_scales, w_words, w_scales, w1, w
         def scatter(u, a, b):
             nc.vector.tensor_copy(out=res[u][:].indirect(offsets[:, a // 16 : b // 16]), in_=z[u][:, a:b])
 
-        def gather_late(c):
-            piece = keep.tile([P, CHUNK], U32, name="gw1", bufs=3, align_bytes=64)
-            gw1.append(piece)
-            cols = slice(c * CHUNK // 16, (c + 1) * CHUNK // 16)
-            nc.vector.tensor_copy(out=piece[:], in_=xw[1][:].bitcast(U32).indirect(offsets[:, cols]))
-
-        early = [first_open(c) for c in range(NE)]
-        for c in range(3):
-            gather_late(c)
+        early = [first_open(c) for c in range(2)]
+        for a, b in ((0, 128), (128, 256), (256, 384), (384, 512)):
+            nc.vector.tensor_copy(out=gw[1][:, a:b], in_=xw[1][:].bitcast(U32).indirect(offsets[:, a // 16 : b // 16]))
         light_close(opened[0], 0, 0)
         first_close(early[0], 0)
-        early.append(first_open(3))
         light_close(opened[1], 0, 1)
         first_close(early[1], 1)
         cast_w2("vector", 0)
-        gather_late(3)
         quantize_w2(0)
-        for c in range(2, 4):
-            first_close(early[c], c)
+        first(2)
+        first(3)
         quantize_h(0)
         copy_z(second(0, 0, 128), 0, 0, 128, "vector")
         quantize_h(1)

@@ -36,7 +36,7 @@ def tile_moe_cas_mlp_relu_kernel(tc, x_words, x_scales, w_words, w_scales, w1, w
         ww1 = keep.tile([P, PASSES, P], I32, name="ww1", align_bytes=64)
         ws = keep.tile([P, PASSES, N], U8, name="ws", align_bytes=64)
         w1_raw = [keep.tile([P, PACK, H], F32, name="w1_raw%d" % s, align_bytes=64) for s in range(PASSES)]
-        w2_raw = [keep.tile([P, PACK, P], F32, name="w2_raw%d" % u, align_bytes=64) for u in range(2)]
+        w2_raw = keep.tile([P, PACK, N], F32, name="w2_raw", align_bytes=64)
         w1_bf = [keep.tile([P, PACK, P, PACK], BF16, name="w1_bf%d" % s, align_bytes=64) for s in range(PASSES)]
         res = [keep.tile([P, T], F32, name="res%d" % u, align_bytes=64) for u in range(2)]
         w1_codes = [keep.tile([P, H], U32, name="w1_codes%d" % s, align_bytes=64) for s in range(PASSES)]
@@ -85,8 +85,6 @@ def tile_moe_cas_mlp_relu_kernel(tc, x_words, x_scales, w_words, w_scales, w1, w
         def load_w1(s):
             nc.sync.dma_start(out=w1_raw[s][:], in_=w1_rows[s])
 
-        def load_w2(u):
-            nc.sync.dma_start(out=w2_raw[u][:], in_=w2_rows[:, :, u * P : (u + 1) * P])
 
         load_x(0)
         nc.sync.dma_start(out=offsets[:], in_=offs)
@@ -104,9 +102,8 @@ def tile_moe_cas_mlp_relu_kernel(tc, x_words, x_scales, w_words, w_scales, w1, w
         for g in range(2):
             words = x_words[1].rearrange("p t d -> p (t d)").bitcast(I32)
             nc.sync.dma_start(out=xw[1][:, g * 512 : (g + 1) * 512], in_=words[:, g * 512 : (g + 1) * 512])
-        load_w2(0)
+        nc.sync.dma_start(out=w2_raw[:], in_=w2_rows)
         load_w_late()
-        load_w2(1)
 
         def cast_w1(engine, dst, raw, t0, t1, m0=0, m1=P):
             dst = dst[:, t0:t1, m0:m1, :].rearrange("p t m j -> p m j t")
@@ -196,7 +193,7 @@ def tile_moe_cas_mlp_relu_kernel(tc, x_words, x_scales, w_words, w_scales, w1, w
 
         def cast_w2(engine, u):
             dst = w2_bf[u][:].rearrange("p (c i) j -> p c j i", i=PACK)
-            src = w2_raw[u][:].rearrange("p j (c i) -> p c j i", i=PACK)
+            src = w2_raw[:, :, u * P : (u + 1) * P].rearrange("p j (c i) -> p c j i", i=PACK)
             if engine == "scalar":
                 nc.scalar.activation(out=dst, in_=src, func=COPY)
             else:

@@ -46,7 +46,9 @@ def tile_moe_cas_mlp_relu_kernel(tc, x_words, x_scales, w_words, w_scales, w1, w
         w2_sc = keep.tile([P, N], U8, name="w2_sc", align_bytes=64)
         gw = [keep.tile([P, S], U32, name="gw%d" % s, align_bytes=64) for s in range(PASSES)]
         gs = keep.tile([P, S], U8, name="gs", align_bytes=64)
-        h_bf = [keep.tile([P, CHUNK, PACK], BF16, name="h_bf%d" % c, align_bytes=64) for c in range(S // CHUNK)]
+        h_late = keep.tile([P, 2 * CHUNK, PACK], BF16, name="h_late", align_bytes=64)
+        h_bf = [keep.tile([P, CHUNK, PACK], BF16, name="h_bf%d" % c, align_bytes=64)[:] for c in range(2)]
+        h_bf.extend([h_late[:, 0:CHUNK, :], h_late[:, CHUNK : 2 * CHUNK, :]])
         h_codes = keep.tile([P, S], U32, name="h_codes", align_bytes=64)
         h_sc = keep.tile([P, S], U8, name="h_sc", align_bytes=64)
         z = [keep.tile([P, S], F32, name="z%d" % u, align_bytes=64) for u in range(2)]
@@ -156,6 +158,17 @@ def tile_moe_cas_mlp_relu_kernel(tc, x_words, x_scales, w_words, w_scales, w1, w
         cast_w1("vector", w1_bf[1][:], w1_raw[1], 2, 4, 0, SHARE)
         quantize_w1(1, 0, 2)
         quantize_w1(1, 2, 4)
+        warm = psum.tile([P, 512], F32, name="acc")
+        for a, b in ((0, 512), (0, 256), (256, 384)):
+            nc.tensor.matmul_mx(
+                out=warm[:, a:b],
+                lhsT=gw[0][:, 0:P].bitcast(FP8X4),
+                lhsT_scale=xs[:, 0:P],
+                rhs=gw[0][:, a:b].bitcast(FP8X4),
+                rhs_scale=xs[:, a:b],
+                start=True,
+                stop=True,
+            )
         opened = [light_open(0, g) for g in range(2)]
 
         def first_pass(acc, c, t, s, start, stop):
@@ -177,7 +190,7 @@ def tile_moe_cas_mlp_relu_kernel(tc, x_words, x_scales, w_words, w_scales, w1, w
             return acc
 
         def relu(acc, c):
-            nc.scalar.activation(out=h_bf[c][:], in_=acc[:].rearrange("p t n -> p n t"), func=RELU)
+            nc.scalar.activation(out=h_bf[c], in_=acc[:].rearrange("p t n -> p n t"), func=RELU)
 
         def first_close(acc, c):
             for t in range(PACK):
@@ -206,7 +219,7 @@ def tile_moe_cas_mlp_relu_kernel(tc, x_words, x_scales, w_words, w_scales, w1, w
         def quantize_h(c):
             slots = slice(c * CHUNK, (c + 1) * CHUNK)
             nc.vector.quantize_mx(
-                out=h_codes[:, slots].bitcast(FP8X4), scales=h_sc[:, slots], in_=h_bf[c][:].rearrange("p n t -> p (n t)")
+                out=h_codes[:, slots].bitcast(FP8X4), scales=h_sc[:, slots], in_=h_bf[c].rearrange("p n t -> p (n t)")
             )
 
         def second(u, a, b):
@@ -239,7 +252,12 @@ def tile_moe_cas_mlp_relu_kernel(tc, x_words, x_scales, w_words, w_scales, w1, w
         def scatter(u, a, b):
             nc.vector.tensor_copy(out=res[u][:].indirect(offsets[:, a // 16 : b // 16]), in_=z[u][:, a:b])
 
-        early = [first_open(c) for c in range(2)]
+        def quantize_h_late():
+            nc.vector.quantize_mx(
+                out=h_codes[:, HALF:S].bitcast(FP8X4), scales=h_sc[:, HALF:S], in_=h_late[:].rearrange("p n t -> p (n t)")
+            )
+
+        early = [first_open(c) for c in range(3)]
         for a, b in ((0, 128), (128, 256), (256, 384), (384, 512)):
             nc.vector.tensor_copy(out=gw[1][:, a:b], in_=xw[1][:].bitcast(U32).indirect(offsets[:, a // 16 : b // 16]))
         light_close(opened[0], 0, 0)
@@ -248,16 +266,15 @@ def tile_moe_cas_mlp_relu_kernel(tc, x_words, x_scales, w_words, w_scales, w1, w
         first_close(early[1], 1)
         cast_w2("vector", 0)
         quantize_w2(0)
-        first(2)
+        first_close(early[2], 2)
         first(3)
         quantize_h(0)
         copy_z(second(0, 0, 128), 0, 0, 128, "vector")
         quantize_h(1)
         cast_w2("vector", 1)
         quantize_w2(1)
-        quantize_h(2)
         scatter(0, 0, 128)
-        quantize_h(3)
+        quantize_h_late()
         late = [light_products(1, 0)]
         copy_z(second(0, 128, 256), 0, 128, 256)
         late.append(light_products(1, 1))

@@ -158,17 +158,6 @@ def tile_moe_cas_mlp_relu_kernel(tc, x_words, x_scales, w_words, w_scales, w1, w
         cast_w1("vector", w1_bf[1][:], w1_raw[1], 2, 4, 0, SHARE)
         quantize_w1(1, 0, 2)
         quantize_w1(1, 2, 4)
-        warm = psum.tile([P, 512], F32, name="acc")
-        for a, b in ((0, 512), (0, 256), (256, 384)):
-            nc.tensor.matmul_mx(
-                out=warm[:, a:b],
-                lhsT=gw[0][:, 0:P].bitcast(FP8X4),
-                lhsT_scale=xs[:, 0:P],
-                rhs=gw[0][:, a:b].bitcast(FP8X4),
-                rhs_scale=xs[:, a:b],
-                start=True,
-                stop=True,
-            )
         opened = [light_open(0, g) for g in range(2)]
 
         def first_pass(acc, c, t, s, start, stop):
@@ -257,7 +246,7 @@ def tile_moe_cas_mlp_relu_kernel(tc, x_words, x_scales, w_words, w_scales, w1, w
                 out=h_codes[:, HALF:S].bitcast(FP8X4), scales=h_sc[:, HALF:S], in_=h_late[:].rearrange("p n t -> p (n t)")
             )
 
-        early = [first_open(c) for c in range(3)]
+        early = [first_open(c) for c in range(2)]
         for a, b in ((0, 128), (128, 256), (256, 384), (384, 512)):
             nc.vector.tensor_copy(out=gw[1][:, a:b], in_=xw[1][:].bitcast(U32).indirect(offsets[:, a // 16 : b // 16]))
         light_close(opened[0], 0, 0)
@@ -266,7 +255,7 @@ def tile_moe_cas_mlp_relu_kernel(tc, x_words, x_scales, w_words, w_scales, w1, w
         first_close(early[1], 1)
         cast_w2("vector", 0)
         quantize_w2(0)
-        first_close(early[2], 2)
+        first(2)
         first(3)
         quantize_h(0)
         copy_z(second(0, 0, 128), 0, 0, 128, "vector")

from contextlib import ExitStack

import concourse.mybir as mybir

K, T, S, H, N = 1024, 1024, 512, 512, 256
FLOPS = 2 * K * N * T + 2 * K * H * S + 2 * H * N * S

F32 = mybir.dt.float32
BF16 = mybir.dt.bfloat16
I32 = mybir.dt.int32
U32 = mybir.dt.uint32
U16 = mybir.dt.uint16
U8 = mybir.dt.uint8
FP8X4 = mybir.dt.float8_e4m3fn_x4
COPY = mybir.ActivationFunctionType.Copy
RELU = mybir.ActivationFunctionType.Relu

P = 128
PACK = 4
PASSES = 2
CHUNK = 128
SHARE = 32
HALF = 256


def tile_moe_cas_mlp_relu_kernel(tc, x_words, x_scales, w_words, w_scales, w1, w2, offs, out):
    nc = tc.nc
    with ExitStack() as ctx:
        keep = ctx.enter_context(tc.tile_pool(name="keep", bufs=1))
        psum = ctx.enter_context(tc.psum_pool(name="psum", bufs=8))

        offsets = keep.tile([P, S // 16], U16, name="offsets")
        xw = [keep.tile([P, T], I32, name="xw%d" % s, align_bytes=64) for s in range(PASSES)]
        xs = keep.tile([P, T], U8, name="xs", align_bytes=64)
        ww0 = [keep.tile([P, P], I32, name="ww0%d" % s, align_bytes=64) for s in range(PASSES)]
        ww1 = keep.tile([P, PASSES, P], I32, name="ww1", align_bytes=64)
        ws = keep.tile([P, PASSES, N], U8, name="ws", align_bytes=64)
        w1_raw = [keep.tile([P, PACK, H], F32, name="w1_raw%d" % s, align_bytes=64) for s in range(PASSES)]
        w2_raw = keep.tile([P, PACK, N], F32, name="w2_raw", align_bytes=64)
        w1_bf = [keep.tile([P, PACK, P, PACK], BF16, name="w1_bf%d" % s, align_bytes=64) for s in range(PASSES)]
        res = [keep.tile([P, T], F32, name="res%d" % u, align_bytes=64) for u in range(2)]
        w1_codes = [keep.tile([P, H], U32, name="w1_codes%d" % s, align_bytes=64) for s in range(PASSES)]
        w1_sc = [keep.tile([P, H], U8, name="w1_sc%d" % s, align_bytes=64) for s in range(PASSES)]
        w2_bf = [keep.tile([P, P, PACK], BF16, name="w2_bf%d" % u, align_bytes=64) for u in range(2)]
        w2_codes = keep.tile([P, N], U32, name="w2_codes", align_bytes=64)
        w2_sc = keep.tile([P, N], U8, name="w2_sc", align_bytes=64)
        gw = [keep.tile([P, S], U32, name="gw%d" % s, align_bytes=64) for s in range(PASSES)]
        gs = keep.tile([P, S], U8, name="gs", align_bytes=64)
        h_late = keep.tile([P, 2 * CHUNK, PACK], BF16, name="h_late", align_bytes=64)
        h_bf = [keep.tile([P, CHUNK, PACK], BF16, name="h_bf%d" % c, align_bytes=64)[:] for c in range(2)]
        h_bf.extend([h_late[:, 0:CHUNK, :], h_late[:, CHUNK : 2 * CHUNK, :]])
        h_codes = keep.tile([P, S], U32, name="h_codes", align_bytes=64)
        h_sc = keep.tile([P, S], U8, name="h_sc", align_bytes=64)
        z = [keep.tile([P, S], F32, name="z%d" % u, align_bytes=64) for u in range(2)]

        nc.vector.memset(xs[:].bitcast(I32), 0)
        nc.vector.memset(ws[:].rearrange("p s n -> p (s n)").bitcast(I32), 0)

        def load_x(s):
            nc.sync.dma_start(out=xw[s][:], in_=x_words[s].rearrange("p t d -> p (t d)").bitcast(I32))

        words_w = w_words.rearrange("s p n d -> p s (n d)").bitcast(I32)

        def load_w0(s):
            nc.sync.dma_start(out=ww0[s][:], in_=words_w[:, s, 0:P])

        def load_w_late():
            nc.sync.dma_start(out=ww1[:], in_=words_w[:, :, P : 2 * P])

        w1_rows = w1.rearrange("(s p j) c -> s p j c", s=PASSES, j=PACK)
        w2_rows = w2.rearrange("(p j) n -> p j n", j=PACK)

        def load_x_scales(q, s):
            row = 32 * q + 4 * s
            nc.sync.dma_start(out=xs[row : row + 4, :].bitcast(I32), in_=x_scales[s, 4 * q : 4 * q + 4, :].bitcast(I32))

        def load_x_scales_both(q):
            nc.sync.dma_start(out=xs[32 * q : 32 * q + 8, :].bitcast(I32), in_=x_scales[:, 4 * q : 4 * q + 4, :].bitcast(I32))

        def load_w_scales():
            for q in range(4):
                nc.sync.dma_start(
                    out=ws[32 * q : 32 * q + 4, :, :].bitcast(I32),
                    in_=w_scales[:, 4 * q : 4 * q + 4, :].rearrange("s r n -> r s n").bitcast(I32),
                )

        def load_w1(s):
            nc.sync.dma_start(out=w1_raw[s][:], in_=w1_rows[s])


        load_x(0)
        nc.sync.dma_start(out=offsets[:], in_=offs)
        for q in range(2):
            load_x_scales_both(q)
        load_x_scales(2, 0)
        load_x_scales(2, 1)
        load_x_scales(3, 0)
        load_w1(0)
        load_x_scales(3, 1)
        load_w_scales()
        load_w0(0)
        load_w1(1)
        load_w0(1)
        for g in range(2):
            words = x_words[1].rearrange("p t d -> p (t d)").bitcast(I32)
            nc.sync.dma_start(out=xw[1][:, g * 512 : (g + 1) * 512], in_=words[:, g * 512 : (g + 1) * 512])
        nc.sync.dma_start(out=w2_raw[:], in_=w2_rows)
        load_w_late()

        def cast_w1(engine, dst, raw, t0, t1, m0=0, m1=P):
            dst = dst[:, t0:t1, m0:m1, :].rearrange("p t m j -> p m j t")
            src = raw[:].rearrange("p j (m t) -> p m j t", t=PACK)[:, m0:m1, :, t0:t1]
            if engine == "scalar":
                nc.scalar.activation(out=dst, in_=src, func=COPY)
            else:
                nc.vector.tensor_copy(out=dst, in_=src)

        def quantize_w1(s, t0, t1):
            cols = slice(t0 * P, t1 * P)
            nc.vector.quantize_mx(
                out=w1_codes[s][:, cols].bitcast(FP8X4),
                scales=w1_sc[s][:, cols],
                in_=w1_bf[s][:, t0:t1, :, :].rearrange("p t m j -> p (t m j)"),
            )

        def light_pass(acc, u, g, s):
            cols = slice(g * 512, (g + 1) * 512)
            nc.tensor.matmul_mx(
                out=acc[:],
                lhsT=(ww0[s][:] if u == 0 else ww1[:, s, :]).bitcast(FP8X4),
                lhsT_scale=ws[:, s, u * P : (u + 1) * P],
                rhs=xw[s][:, cols].bitcast(FP8X4),
                rhs_scale=xs[4 * s : P, cols],
                start=(s == 0),
                stop=(s == PASSES - 1),
            )

        def light_open(u, g):
            acc = psum.tile([P, 512], F32, name="acc")
            light_pass(acc, u, g, 0)
            return acc

        def light_close(acc, u, g):
            light_pass(acc, u, g, 1)
            nc.scalar.activation(out=res[u][:, g * 512 : (g + 1) * 512], in_=acc[:], func=COPY)

        def cast_shared(dst, raw):
            cast_w1("vector", dst, raw, 0, 2)
            cast_w1("scalar", dst, raw, 2, 4)

        nc.vector.tensor_copy(out=gw[0][:], in_=xw[0][:].bitcast(U32).indirect(offsets[:]))
        nc.vector.tensor_copy(out=gs[:], in_=xs[:].indirect(offsets[:]))
        cast_shared(w1_bf[0][:], w1_raw[0])
        quantize_w1(0, 0, 2)
        quantize_w1(0, 2, 4)
        cast_w1("vector", w1_bf[1][:], w1_raw[1], 0, 2)
        cast_w1("scalar", w1_bf[1][:], w1_raw[1], 2, 4, SHARE, P)
        cast_w1("vector", w1_bf[1][:], w1_raw[1], 2, 4, 0, SHARE)
        quantize_w1(1, 0, 2)
        quantize_w1(1, 2, 4)
        opened = [light_open(0, g) for g in range(2)]

        def first_pass(acc, c, t, s, start, stop):
            slots = slice(c * CHUNK, (c + 1) * CHUNK)
            nc.tensor.matmul_mx(
                out=acc[:, t, :],
                lhsT=w1_codes[s][:, t * P : (t + 1) * P].bitcast(FP8X4),
                lhsT_scale=w1_sc[s][:, t * P : (t + 1) * P],
                rhs=gw[s][:, slots].bitcast(FP8X4),
                rhs_scale=gs[4 * s : P, slots],
                start=start,
                stop=stop,
            )

        def first_open(c):
            acc = psum.tile([P, PACK, CHUNK], F32, name="acc")
            for t in range(PACK):
                first_pass(acc, c, t, 0, t == 0, False)
            return acc

        def relu(acc, c):
            nc.scalar.activation(out=h_bf[c], in_=acc[:].rearrange("p t n -> p n t"), func=RELU)

        def first_close(acc, c):
            for t in range(PACK):
                first_pass(acc, c, t, 1, False, t == PACK - 1)
            relu(acc, c)

        def first(c):
            acc = psum.tile([P, PACK, CHUNK], F32, name="acc")
            for t in range(PACK):
                for s in (1, 0):
                    first_pass(acc, c, t, s, s == 1, s == 0)
            relu(acc, c)

        def cast_w2(engine, u):
            dst = w2_bf[u][:].rearrange("p (c i) j -> p c j i", i=PACK)
            src = w2_raw[:, :, u * P : (u + 1) * P].rearrange("p j (c i) -> p c j i", i=PACK)
            if engine == "scalar":
                nc.scalar.activation(out=dst, in_=src, func=COPY)
            else:
                nc.vector.tensor_copy(out=dst, in_=src)

        def quantize_w2(u):
            cols = slice(u * P, (u + 1) * P)
            nc.vector.quantize_mx(out=w2_codes[:, cols].bitcast(FP8X4), scales=w2_sc[:, cols], in_=w2_bf[u][:].rearrange("p n j -> p (n j)"))

        def quantize_h(c):
            slots = slice(c * CHUNK, (c + 1) * CHUNK)
            nc.vector.quantize_mx(
                out=h_codes[:, slots].bitcast(FP8X4), scales=h_sc[:, slots], in_=h_bf[c].rearrange("p n t -> p (n t)")
            )

        def second(u, a, b):
            acc = psum.tile([P, b - a], F32, name="acc")
            nc.tensor.matmul_mx(
                out=acc[:],
                lhsT=w2_codes[:, u * P : (u + 1) * P].bitcast(FP8X4),
                lhsT_scale=w2_sc[:, u * P : (u + 1) * P],
                rhs=h_codes[:, a:b].bitcast(FP8X4),
                rhs_scale=h_sc[:, a:b],
                start=True,
                stop=True,
            )
            return acc

        def copy_z(acc, u, a, b, engine="scalar"):
            if engine == "scalar":
                nc.scalar.activation(out=z[u][:, a:b], in_=acc[:], func=COPY)
            else:
                nc.vector.tensor_copy(out=z[u][:, a:b], in_=acc[:])

        def light_products(u, g):
            acc = light_open(u, g)
            light_pass(acc, u, g, 1)
            return acc

        def light_copy(acc, u, g):
            nc.scalar.activation(out=res[u][:, g * 512 : (g + 1) * 512], in_=acc[:], func=COPY)

        def scatter(u, a, b):
            nc.vector.tensor_copy(out=res[u][:].indirect(offsets[:, a // 16 : b // 16]), in_=z[u][:, a:b])

        def quantize_h_late():
            nc.vector.quantize_mx(
                out=h_codes[:, HALF:S].bitcast(FP8X4), scales=h_sc[:, HALF:S], in_=h_late[:].rearrange("p n t -> p (n t)")
            )

        early = [first_open(c) for c in range(2)]
        for a, b in ((0, 128), (128, 256), (256, 384), (384, 512)):
            nc.vector.tensor_copy(out=gw[1][:, a:b], in_=xw[1][:].bitcast(U32).indirect(offsets[:, a // 16 : b // 16]))
        light_close(opened[0], 0, 0)
        first_close(early[0], 0)
        light_close(opened[1], 0, 1)
        first_close(early[1], 1)
        cast_w2("vector", 0)
        quantize_w2(0)
        first(2)
        first(3)
        quantize_h(0)
        copy_z(second(0, 0, 128), 0, 0, 128, "vector")
        quantize_h(1)
        cast_w2("vector", 1)
        quantize_w2(1)
        scatter(0, 0, 128)
        quantize_h_late()
        late = [light_products(1, 0)]
        copy_z(second(0, 128, 256), 0, 128, 256)
        late.append(light_products(1, 1))
        scatter(0, 128, 256)
        for g in range(2):
            light_copy(late[g], 1, g)
        copy_z(second(1, 0, 128), 1, 0, 128)
        scatter(1, 0, 128)
        copy_z(second(0, 256, 512), 0, 256, 512)
        scatter(0, 256, 512)
        nc.sync.dma_start(out=out[0:P, :], in_=res[0][:])
        copy_z(second(1, 128, 256), 1, 128, 256)
        copy_z(second(1, 256, 512), 1, 256, 512)
        scatter(1, 128, 512)
        nc.sync.dma_start(out=out[P : 2 * P, :], in_=res[1][:])
